import numpy as np
import ml_dtypes


def mxq(x, axis, fmt="e4m3"):
    dtype, down = {"e4m3": (ml_dtypes.float8_e4m3fn, 7), "e5m2": (ml_dtypes.float8_e5m2, 14)}[fmt]
    v = np.moveaxis(np.asarray(x, np.float32).astype(ml_dtypes.bfloat16).astype(np.float64), axis, -1)
    blocks = v.reshape(v.shape[:-1] + (-1, 32))
    amax = np.abs(blocks).max(-1, keepdims=True)
    byte = np.maximum(np.where(amax > 0, np.frexp(amax)[1] - 1 + 127, 0) - down, 1)
    scale = np.exp2(byte - 127.0)
    codes = (blocks / scale).astype(np.float32).astype(dtype).astype(np.float64)
    return np.moveaxis((codes * scale).reshape(v.shape), -1, axis)


WIDE = False


def mx_kscale(k):
    if not WIDE:
        return np.ones(k)
    levels = np.array([10, -10, 5, -5, 0])
    if k % 512:
        return np.exp2(np.random.permutation(np.resize(levels, k // 32))).repeat(32)
    a = np.empty((k // 512, 16))
    for p in range(k // 512):
        a[p, :8] = np.random.permutation(np.resize(levels, 8))
        for g in range(8):
            far = levels[np.abs(levels - a[p, g]) >= 10]
            a[p, g + 8] = far[np.random.randint(len(far))]
    return np.exp2(a.ravel()).repeat(32)


def f64(x):
    return np.asarray(x).astype(np.float64)


def striped(idx):
    return np.tile(idx.reshape(-1, 16).T, (8, 1)).astype(np.uint16)


def unstriped(offs):
    return offs[:16].T.reshape(-1).astype(np.int64)


def pack_weight(w):
    k, n = w.shape
    w = f64(np.asarray(w, np.float32).astype(ml_dtypes.bfloat16)).reshape(k // 32, 32, n)
    amax = np.abs(w).max(1)
    byte = np.clip(np.where(amax > 0, np.frexp(amax)[1] - 1 + 127 - 7, 1), 1, 254)
    scaled = (w * np.exp2(127.0 - byte)[:, None, :]).reshape(k, n).astype(np.float32)
    words = np.ascontiguousarray(scaled.reshape(k // 512, 128, 4, n).transpose(0, 1, 3, 2)).astype(ml_dtypes.float8_e4m3fn).view(np.uint8)
    return words, np.ascontiguousarray(byte.astype(np.uint8).reshape(k // 512, 16, n))


def unpack_weight(words, scales):
    g, p, n, _ = words.shape
    vals = np.ascontiguousarray(words).view(ml_dtypes.float8_e4m3fn).astype(np.float64) * np.repeat(np.exp2(scales.astype(np.float64) - 127.0), 8, axis=1)[..., None]
    return vals.transpose(0, 1, 3, 2).reshape(g * 512, n)


def relu(v):
    return np.maximum(v, 0.0)


def sigmoid(v):
    return 1.0 / (1.0 + np.exp(-np.maximum(v, -700.0)))


K, T, S, N, V = 512, 2048, 512, 128, 256


def setup_inputs():
    n = np.random.standard_normal
    s = mx_kscale(K)[:, None]
    packed_xT = pack_weight(n((K, T)) * s)
    return {
        "x_words": packed_xT[0],
        "x_scales": packed_xT[1],
        "w1": (n((K, N)) / np.sqrt(K) / s).astype(np.float32),
        "recv": (np.random.uniform(0.6, 2.0, (N, V))).astype(np.float32),
        "soft": (np.random.uniform(0.2, 0.8, (N, 1))).astype(np.float32),
        "offs": striped(np.random.permutation(T)[:S]),
        "pos1": striped(np.random.permutation(S)[:V]),
        "pos2": striped(np.random.permutation(S)[:V]),
        "pos3": striped(np.random.permutation(S)[:V]),
        "pos4": striped(np.random.permutation(S)[:V]),
    }


def reference(x_words, x_scales, w1, recv, soft, offs, pos1, pos2, pos3, pos4):
    xq = unpack_weight(x_words, x_scales)[:, unstriped(offs)]
    y = mxq(f64(w1), 0, "e4m3").T @ xq
    dep = np.log(np.exp(y) + 1.0) + 0.3
    g0 = dep[:, unstriped(pos1)]
    bk0 = sigmoid(6.0 * (f64(recv) - g0))
    g1 = dep[:, unstriped(pos2)]
    bk1 = sigmoid(6.0 * (f64(recv) - g1))
    g2 = dep[:, unstriped(pos3)]
    bk2 = sigmoid(6.0 * (f64(recv) - g2))
    g3 = dep[:, unstriped(pos4)]
    bk3 = sigmoid(6.0 * (f64(recv) - g3))
    nblk = bk0 + bk1 + bk2 + bk3 + 0.1
    avg = (bk0 * g0 + bk1 * g1 + bk2 * g2 + bk3 * g3) / nblk
    pen = 0.8 * ((relu(f64(recv) - avg)) / (avg + 0.1)) + 0.15
    return pen * nblk - (f64(soft) * (np.abs(f64(recv) - avg)))

@@ -1,0 +1,159 @@
+from contextlib import ExitStack
+
+import concourse.mybir as mybir
+
+K, T, S, N, V = 512, 2048, 512, 128, 256
+FLOPS = 2 * K * S * N
+
+F32 = mybir.dt.float32
+BF16 = mybir.dt.bfloat16
+I32 = mybir.dt.int32
+U32 = mybir.dt.uint32
+U16 = mybir.dt.uint16
+U8 = mybir.dt.uint8
+FP8X4 = mybir.dt.float8_e4m3fn_x4
+ALU = mybir.AluOpType
+ACT = mybir.ActivationFunctionType
+
+P = 128
+PACK = 4
+HALF = S // 2
+LINEAR_FROM = 30.0
+
+
+def tile_picked_ypcss_pen_p_kernel(
+    tc, x_words, x_scales, w1, recv, soft, offs, pos1, pos2, pos3, pos4, out
+):
+    nc = tc.nc
+    with ExitStack() as ctx:
+        lists = ctx.enter_context(tc.tile_pool(name="lists", bufs=1))
+        keep = ctx.enter_context(tc.tile_pool(name="keep", bufs=1))
+        psum = ctx.enter_context(tc.psum_pool(name="psum", bufs=1))
+
+        scale_table = keep.tile([P, T], U8, name="scale_table", align_bytes=64)
+        nc.vector.memset(scale_table[:].bitcast(I32), 0)
+        w_rows = keep.tile([P, PACK, N], F32, name="w_rows", tag="first")
+        nc.sync.dma_start(w_rows[:], w1.rearrange("(p j) m -> p j m", j=PACK))
+        for q in range(4):
+            nc.sync.dma_start(
+                scale_table[32 * q : 32 * q + 4, :].bitcast(I32),
+                x_scales[0, 4 * q : 4 * q + 4, :].bitcast(I32),
+            )
+
+        picked = lists.tile([P, S // 16], U16, name="picked")
+        nc.sync.dma_start(picked[:], offs)
+        word_table = keep.tile([P, T], U32, name="word_table", align_bytes=64)
+        nc.sync.dma_start(
+            word_table[:].bitcast(I32),
+            x_words[0].rearrange("p n t -> p (n t)").bitcast(I32),
+        )
+
+        w_bf16 = keep.tile([P, N, PACK], BF16, name="w_bf16", tag="staged", align_bytes=64)
+        nc.vector.tensor_copy(
+            w_bf16[:].rearrange("p (c i) j -> p c j i", i=4),
+            w_rows[:].rearrange("p j (c i) -> p c j i", i=4),
+        )
+        w_codes = keep.tile([P, N], U32, name="w_codes", align_bytes=64)
+        w_scales = keep.tile([P, N], U8, name="w_scales", align_bytes=64)
+        nc.vector.quantize_mx(
+            out=w_codes[:].bitcast(FP8X4),
+            scales=w_scales[:],
+            in_=w_bf16[:].rearrange("p m j -> p (m j)"),
+        )
+
+        x_scale = keep.tile([P, S], U8, name="x_scale", align_bytes=64)
+        nc.vector.tensor_copy(x_scale[:], scale_table[:].indirect(picked[:]))
+
+        seen = []
+        for i, pos in enumerate((pos1, pos2, pos3, pos4)):
+            tile = lists.tile([P, V // 16], U16, name="seen%d" % i)
+            nc.sync.dma_start(tile[:], pos)
+            seen.append(tile)
+        r = keep.tile([P, V], F32, name="r", tag="staged", align_bytes=64)
+        nc.sync.dma_start(r[:], recv)
+        softness = keep.tile([P, 1], F32, name="softness", tag="first")
+        nc.sync.dma_start(softness[:], soft)
+
+        exp_y = keep.tile([P, S], F32, name="exp_y")
+        y = []
+        for h in range(2):
+            cols = slice(h * HALF, (h + 1) * HALF)
+            codes = keep.tile([P, HALF], U32, name="x_codes%d" % h, align_bytes=64)
+            nc.vector.tensor_copy(
+                codes[:], word_table[:].indirect(picked[:, h * HALF // 16 : (h + 1) * HALF // 16])
+            )
+            bank = psum.tile([P, HALF], F32, name="y%d" % h)
+            nc.tensor.matmul_mx(
+                out=bank[:],
+                lhsT=w_codes[:].bitcast(FP8X4),
+                lhsT_scale=w_scales[:],
+                rhs=codes[:].bitcast(FP8X4),
+                rhs_scale=x_scale[:, cols],
+                start=True,
+                stop=True,
+            )
+            nc.scalar.activation(exp_y[:, cols], bank[:], ACT.Exp)
+            y.append(bank)
+
+        log1p = keep.tile([P, S], F32, name="log1p")
+        softplus = keep.tile([P, S], F32, name="softplus")
+        for h in range(2):
+            cols = slice(h * HALF, (h + 1) * HALF)
+            nc.scalar.activation(log1p[:, cols], exp_y[:, cols], ACT.Ln, bias=1.0)
+            nc.vector.scalar_tensor_tensor(
+                softplus[:, cols], log1p[:, cols], LINEAR_FROM, y[h][:], ALU.min, ALU.max
+            )
+
+        terms = []
+        for i in range(4):
+            gap = keep.tile([P, V], F32, name="gap%d" % i)
+            nc.vector.tensor_tensor(gap[:], softplus[:].indirect(seen[i][:]), r[:], ALU.subtract)
+            both = keep.tile([P, 2, V], F32, name="both%d" % i)
+            if i < 3:
+                nc.scalar.activation(both[:, 1, :], gap[:], ACT.Silu, scale=-6.0, bias=-1.8)
+                nc.scalar.activation(both[:, 0, :], gap[:], ACT.Tanh, scale=-3.0, bias=-0.9)
+            else:
+                nc.scalar.activation(both[:, 0, :], gap[:], ACT.Tanh, scale=-3.0, bias=-0.9)
+                nc.scalar.activation(both[:, 1, :], gap[:], ACT.Silu, scale=-6.0, bias=-1.8)
+            terms.append(both)
+
+        def work(name):
+            return keep.tile([P, V], F32, name=name)
+
+        sum01 = keep.tile([P, 2, V], F32, name="sum01")
+        nc.vector.tensor_tensor(sum01[:], terms[0][:], terms[1][:], ALU.add)
+        sum012 = keep.tile([P, 2, V], F32, name="sum012")
+        nc.vector.tensor_tensor(sum012[:], sum01[:], terms[2][:], ALU.add)
+        e_part = work("e_part")
+        nc.vector.scalar_tensor_tensor(e_part[:], r[:], 0.6, sum012[:, 1, :], ALU.mult, ALU.add)
+        n2 = work("n2")
+        nc.vector.scalar_tensor_tensor(n2[:], sum012[:, 0, :], 4.2, terms[3][:, 0, :], ALU.add, ALU.add)
+        e6 = work("e6")
+        nc.vector.tensor_tensor(e6[:], e_part[:], terms[3][:, 1, :], ALU.add)
+        m2 = work("m2")
+        nc.vector.scalar_tensor_tensor(m2[:], r[:], 0.1, n2[:], ALU.add, ALU.mult)
+        w6 = work("w6")
+        nc.vector.scalar_tensor_tensor(w6[:], m2[:], 3.0, e6[:], ALU.mult, ALU.subtract)
+        neg_abs = work("neg_abs")
+        nc.vector.scalar_tensor_tensor(neg_abs[:], e6[:], -1.0, e6[:], ALU.mult, ALU.min)
+        front = work("front")
+        nc.vector.scalar_tensor_tensor(front[:], e6[:], 0.0, n2[:], ALU.max, ALU.mult)
+
+        rs_n = work("rs_n")
+        nc.scalar.activation(rs_n[:], n2[:], ACT.Abs_reciprocal_sqrt, scale=0.225)
+        rs_w = work("rs_w")
+        nc.scalar.activation(rs_w[:], w6[:], ACT.Abs_reciprocal_sqrt, scale=2.5)
+        inv_n = work("inv_n")
+        nc.scalar.activation(inv_n[:], rs_n[:], ACT.Square)
+        inv_w = work("inv_w")
+        nc.scalar.activation(inv_w[:], rs_w[:], ACT.Square)
+
+        dist = work("dist")
+        nc.vector.tensor_tensor(dist[:], neg_abs[:], inv_n[:], ALU.mult)
+        width = work("width")
+        nc.vector.tensor_tensor(width[:], front[:], inv_w[:], ALU.mult)
+        rest = work("rest")
+        nc.vector.scalar_tensor_tensor(rest[:], dist[:], softness[:], n2[:], ALU.mult, ALU.add)
+        result = work("result")
+        nc.vector.scalar_tensor_tensor(result[:], rest[:], 0.075, width[:], ALU.mult, ALU.add)
+        nc.sync.dma_start(out, result[:])

@@ -19,6 +19,7 @@ P = 128
 PACK = 4
 HALF = S // 2
 LINEAR_FROM = 30.0
+EARLY = T // 4
 
 
 def tile_picked_ypcss_pen_p_kernel(
@@ -34,6 +35,9 @@ def tile_picked_ypcss_pen_p_kernel(
         nc.vector.memset(scale_table[:].bitcast(I32), 0)
         w_rows = keep.tile([P, PACK, N], F32, name="w_rows", tag="first")
         nc.sync.dma_start(w_rows[:], w1.rearrange("(p j) m -> p j m", j=PACK))
+        word_table = keep.tile([P, T], U32, name="word_table", align_bytes=64)
+        words = x_words[0].rearrange("p n t -> p (n t)").bitcast(I32)
+        nc.sync.dma_start(word_table[:, :EARLY].bitcast(I32), words[:, :EARLY])
         for q in range(4):
             nc.sync.dma_start(
                 scale_table[32 * q : 32 * q + 4, :].bitcast(I32),
@@ -42,11 +46,7 @@ def tile_picked_ypcss_pen_p_kernel(
 
         picked = lists.tile([P, S // 16], U16, name="picked")
         nc.sync.dma_start(picked[:], offs)
-        word_table = keep.tile([P, T], U32, name="word_table", align_bytes=64)
-        nc.sync.dma_start(
-            word_table[:].bitcast(I32),
-            x_words[0].rearrange("p n t -> p (n t)").bitcast(I32),
-        )
+        nc.sync.dma_start(word_table[:, EARLY:].bitcast(I32), words[:, EARLY:])
 
         w_bf16 = keep.tile([P, N, PACK], BF16, name="w_bf16", tag="staged", align_bytes=64)
         nc.vector.tensor_copy(
@@ -95,65 +95,56 @@ def tile_picked_ypcss_pen_p_kernel(
             nc.scalar.activation(exp_y[:, cols], bank[:], ACT.Exp)
             y.append(bank)
 
-        log1p = keep.tile([P, S], F32, name="log1p")
-        softplus = keep.tile([P, S], F32, name="softplus")
-        for h in range(2):
-            cols = slice(h * HALF, (h + 1) * HALF)
-            nc.scalar.activation(log1p[:, cols], exp_y[:, cols], ACT.Ln, bias=1.0)
-            nc.vector.scalar_tensor_tensor(
-                softplus[:, cols], log1p[:, cols], LINEAR_FROM, y[h][:], ALU.min, ALU.max
-            )
-
-        terms = []
-        for i in range(4):
-            gap = keep.tile([P, V], F32, name="gap%d" % i)
-            nc.vector.tensor_tensor(gap[:], softplus[:].indirect(seen[i][:]), r[:], ALU.subtract)
-            both = keep.tile([P, 2, V], F32, name="both%d" % i)
-            if i < 3:
-                nc.scalar.activation(both[:, 1, :], gap[:], ACT.Silu, scale=-6.0, bias=-1.8)
-                nc.scalar.activation(both[:, 0, :], gap[:], ACT.Tanh, scale=-3.0, bias=-0.9)
-            else:
-                nc.scalar.activation(both[:, 0, :], gap[:], ACT.Tanh, scale=-3.0, bias=-0.9)
-                nc.scalar.activation(both[:, 1, :], gap[:], ACT.Silu, scale=-6.0, bias=-1.8)
-            terms.append(both)
-
         def work(name):
             return keep.tile([P, V], F32, name=name)
 
-        sum01 = keep.tile([P, 2, V], F32, name="sum01")
-        nc.vector.tensor_tensor(sum01[:], terms[0][:], terms[1][:], ALU.add)
-        sum012 = keep.tile([P, 2, V], F32, name="sum012")
-        nc.vector.tensor_tensor(sum012[:], sum01[:], terms[2][:], ALU.add)
-        e_part = work("e_part")
-        nc.vector.scalar_tensor_tensor(e_part[:], r[:], 0.6, sum012[:, 1, :], ALU.mult, ALU.add)
-        n2 = work("n2")
-        nc.vector.scalar_tensor_tensor(n2[:], sum012[:, 0, :], 4.2, terms[3][:, 0, :], ALU.add, ALU.add)
-        e6 = work("e6")
-        nc.vector.tensor_tensor(e6[:], e_part[:], terms[3][:, 1, :], ALU.add)
-        m2 = work("m2")
+
+        log1p = keep.tile([P, S], F32, name="log1p")
+        softplus = keep.tile([P, S], F32, name="softplus")
+        for h, c0, c1 in ((0, 0, HALF // 2), (0, HALF // 2, HALF), (1, 0, HALF)):
+            cols = slice(h * HALF + c0, h * HALF + c1)
+            nc.scalar.activation(log1p[:, cols], exp_y[:, cols], ACT.Ln, bias=1.0)
+            nc.vector.scalar_tensor_tensor(
+                softplus[:, cols], log1p[:, cols], LINEAR_FROM, y[h][:, c0:c1], ALU.min, ALU.max
+            )
+
+        tanh, silu = [], []
+        for i in range(4):
+            gap = work("gap%d" % i)
+            nc.vector.tensor_tensor(gap[:], softplus[:].indirect(seen[i][:]), r[:], ALU.subtract)
+            tanh.append(work("tanh%d" % i))
+            silu.append(work("silu%d" % i))
+            calls = [(silu[i], ACT.Silu, -6.0), (tanh[i], ACT.Tanh, -3.0)]
+            for dst, func, scale in calls if i < 3 else reversed(calls):
+                nc.scalar.activation(dst[:], gap[:], func, scale=scale, bias=0.3 * scale)
+
+        e0, e1, e2, e6 = work("e0"), work("e1"), work("e2"), work("e6")
+        t1, t2, n2, m2, w6 = work("t1"), work("t2"), work("n2"), work("m2"), work("w6")
+        n_sq, neg_abs, front = work("n_sq"), work("neg_abs"), work("front")
+        nc.vector.scalar_tensor_tensor(e0[:], r[:], 0.6, silu[0][:], ALU.mult, ALU.add)
+        nc.vector.tensor_tensor(t1[:], tanh[0][:], tanh[1][:], ALU.add)
+        nc.vector.tensor_tensor(e1[:], e0[:], silu[1][:], ALU.add)
+        nc.vector.tensor_tensor(t2[:], t1[:], tanh[2][:], ALU.add)
+        nc.vector.tensor_tensor(e2[:], e1[:], silu[2][:], ALU.add)
+        nc.vector.scalar_tensor_tensor(n2[:], t2[:], 4.2, tanh[3][:], ALU.add, ALU.add)
+        nc.vector.tensor_tensor(e6[:], e2[:], silu[3][:], ALU.add)
         nc.vector.scalar_tensor_tensor(m2[:], r[:], 0.1, n2[:], ALU.add, ALU.mult)
-        w6 = work("w6")
+        nc.vector.tensor_tensor(n_sq[:], n2[:], n2[:], ALU.mult)
         nc.vector.scalar_tensor_tensor(w6[:], m2[:], 3.0, e6[:], ALU.mult, ALU.subtract)
-        neg_abs = work("neg_abs")
         nc.vector.scalar_tensor_tensor(neg_abs[:], e6[:], -1.0, e6[:], ALU.mult, ALU.min)
-        front = work("front")
         nc.vector.scalar_tensor_tensor(front[:], e6[:], 0.0, n2[:], ALU.max, ALU.mult)
 
-        rs_n = work("rs_n")
-        nc.scalar.activation(rs_n[:], n2[:], ACT.Abs_reciprocal_sqrt, scale=0.225)
-        rs_w = work("rs_w")
+        inv_n, rs_w, inv_w = work("inv_n"), work("rs_w"), work("inv_w")
+        nc.scalar.activation(inv_n[:], n_sq[:], ACT.Abs_reciprocal_sqrt, scale=0.225 * 0.225)
         nc.scalar.activation(rs_w[:], w6[:], ACT.Abs_reciprocal_sqrt, scale=2.5)
-        inv_n = work("inv_n")
-        nc.scalar.activation(inv_n[:], rs_n[:], ACT.Square)
-        inv_w = work("inv_w")
         nc.scalar.activation(inv_w[:], rs_w[:], ACT.Square)
 
-        dist = work("dist")
+        dist, rest, width, result = work("dist"), work("rest"), work("width"), work("result")
         nc.vector.tensor_tensor(dist[:], neg_abs[:], inv_n[:], ALU.mult)
-        width = work("width")
-        nc.vector.tensor_tensor(width[:], front[:], inv_w[:], ALU.mult)
-        rest = work("rest")
         nc.vector.scalar_tensor_tensor(rest[:], dist[:], softness[:], n2[:], ALU.mult, ALU.add)
-        result = work("result")
-        nc.vector.scalar_tensor_tensor(result[:], rest[:], 0.075, width[:], ALU.mult, ALU.add)
+        halves = [slice(0, V // 2), slice(V // 2, V)]
+        for cols in halves:
+            nc.vector.tensor_tensor(width[:, cols], front[:, cols], inv_w[:, cols], ALU.mult)
+        for cols in halves:
+            nc.vector.scalar_tensor_tensor(result[:, cols], rest[:, cols], 0.075, width[:, cols], ALU.mult, ALU.add)
         nc.sync.dma_start(out, result[:])

from contextlib import ExitStack

import concourse.mybir as mybir

K, T, S, N, V = 512, 2048, 512, 128, 256
FLOPS = 2 * K * S * N

F32 = mybir.dt.float32
BF16 = mybir.dt.bfloat16
I32 = mybir.dt.int32
U32 = mybir.dt.uint32
U16 = mybir.dt.uint16
U8 = mybir.dt.uint8
FP8X4 = mybir.dt.float8_e4m3fn_x4
ALU = mybir.AluOpType
ACT = mybir.ActivationFunctionType

P = 128
PACK = 4
HALF = S // 2
LINEAR_FROM = 30.0
EARLY = T // 4


def tile_picked_ypcss_pen_p_kernel(
    tc, x_words, x_scales, w1, recv, soft, offs, pos1, pos2, pos3, pos4, out
):
    nc = tc.nc
    with ExitStack() as ctx:
        lists = ctx.enter_context(tc.tile_pool(name="lists", bufs=1))
        keep = ctx.enter_context(tc.tile_pool(name="keep", bufs=1))
        psum = ctx.enter_context(tc.psum_pool(name="psum", bufs=1))

        scale_table = keep.tile([P, T], U8, name="scale_table", align_bytes=64)
        nc.vector.memset(scale_table[:].bitcast(I32), 0)
        w_rows = keep.tile([P, PACK, N], F32, name="w_rows", tag="first")
        nc.sync.dma_start(w_rows[:], w1.rearrange("(p j) m -> p j m", j=PACK))
        word_table = keep.tile([P, T], U32, name="word_table", align_bytes=64)
        words = x_words[0].rearrange("p n t -> p (n t)").bitcast(I32)
        nc.sync.dma_start(word_table[:, :EARLY].bitcast(I32), words[:, :EARLY])
        for q in range(4):
            nc.sync.dma_start(
                scale_table[32 * q : 32 * q + 4, :].bitcast(I32),
                x_scales[0, 4 * q : 4 * q + 4, :].bitcast(I32),
            )

        picked = lists.tile([P, S // 16], U16, name="picked")
        nc.sync.dma_start(picked[:], offs)
        nc.sync.dma_start(word_table[:, EARLY:].bitcast(I32), words[:, EARLY:])

        w_bf16 = keep.tile([P, N, PACK], BF16, name="w_bf16", tag="staged", align_bytes=64)
        nc.vector.tensor_copy(
            w_bf16[:].rearrange("p (c i) j -> p c j i", i=4),
            w_rows[:].rearrange("p j (c i) -> p c j i", i=4),
        )
        w_codes = keep.tile([P, N], U32, name="w_codes", align_bytes=64)
        w_scales = keep.tile([P, N], U8, name="w_scales", align_bytes=64)
        nc.vector.quantize_mx(
            out=w_codes[:].bitcast(FP8X4),
            scales=w_scales[:],
            in_=w_bf16[:].rearrange("p m j -> p (m j)"),
        )

        x_scale = keep.tile([P, S], U8, name="x_scale", align_bytes=64)
        nc.vector.tensor_copy(x_scale[:], scale_table[:].indirect(picked[:]))

        seen = []
        for i, pos in enumerate((pos1, pos2, pos3, pos4)):
            tile = lists.tile([P, V // 16], U16, name="seen%d" % i)
            nc.sync.dma_start(tile[:], pos)
            seen.append(tile)
        r = keep.tile([P, V], F32, name="r", tag="staged", align_bytes=64)
        nc.sync.dma_start(r[:], recv)
        softness = keep.tile([P, 1], F32, name="softness", tag="first")
        nc.sync.dma_start(softness[:], soft)

        exp_y = keep.tile([P, S], F32, name="exp_y")
        y = []
        for h in range(2):
            cols = slice(h * HALF, (h + 1) * HALF)
            codes = keep.tile([P, HALF], U32, name="x_codes%d" % h, align_bytes=64)
            nc.vector.tensor_copy(
                codes[:], word_table[:].indirect(picked[:, h * HALF // 16 : (h + 1) * HALF // 16])
            )
            bank = psum.tile([P, HALF], F32, name="y%d" % h)
            nc.tensor.matmul_mx(
                out=bank[:],
                lhsT=w_codes[:].bitcast(FP8X4),
                lhsT_scale=w_scales[:],
                rhs=codes[:].bitcast(FP8X4),
                rhs_scale=x_scale[:, cols],
                start=True,
                stop=True,
            )
            nc.scalar.activation(exp_y[:, cols], bank[:], ACT.Exp)
            y.append(bank)

        def work(name):
            return keep.tile([P, V], F32, name=name)


        log1p = keep.tile([P, S], F32, name="log1p")
        softplus = keep.tile([P, S], F32, name="softplus")
        for h, c0, c1 in ((0, 0, HALF // 2), (0, HALF // 2, HALF), (1, 0, HALF)):
            cols = slice(h * HALF + c0, h * HALF + c1)
            nc.scalar.activation(log1p[:, cols], exp_y[:, cols], ACT.Ln, bias=1.0)
            nc.vector.scalar_tensor_tensor(
                softplus[:, cols], log1p[:, cols], LINEAR_FROM, y[h][:, c0:c1], ALU.min, ALU.max
            )

        tanh, silu = [], []
        for i in range(4):
            gap = work("gap%d" % i)
            nc.vector.tensor_tensor(gap[:], softplus[:].indirect(seen[i][:]), r[:], ALU.subtract)
            tanh.append(work("tanh%d" % i))
            silu.append(work("silu%d" % i))
            calls = [(silu[i], ACT.Silu, -6.0), (tanh[i], ACT.Tanh, -3.0)]
            for dst, func, scale in calls if i < 3 else reversed(calls):
                nc.scalar.activation(dst[:], gap[:], func, scale=scale, bias=0.3 * scale)

        e0, e1, e2, e6 = work("e0"), work("e1"), work("e2"), work("e6")
        t1, t2, n2, m2, w6 = work("t1"), work("t2"), work("n2"), work("m2"), work("w6")
        n_sq, neg_abs, front = work("n_sq"), work("neg_abs"), work("front")
        nc.vector.scalar_tensor_tensor(e0[:], r[:], 0.6, silu[0][:], ALU.mult, ALU.add)
        nc.vector.tensor_tensor(t1[:], tanh[0][:], tanh[1][:], ALU.add)
        nc.vector.tensor_tensor(e1[:], e0[:], silu[1][:], ALU.add)
        nc.vector.tensor_tensor(t2[:], t1[:], tanh[2][:], ALU.add)
        nc.vector.tensor_tensor(e2[:], e1[:], silu[2][:], ALU.add)
        nc.vector.scalar_tensor_tensor(n2[:], t2[:], 4.2, tanh[3][:], ALU.add, ALU.add)
        nc.vector.tensor_tensor(e6[:], e2[:], silu[3][:], ALU.add)
        nc.vector.scalar_tensor_tensor(m2[:], r[:], 0.1, n2[:], ALU.add, ALU.mult)
        nc.vector.tensor_tensor(n_sq[:], n2[:], n2[:], ALU.mult)
        nc.vector.scalar_tensor_tensor(w6[:], m2[:], 3.0, e6[:], ALU.mult, ALU.subtract)
        nc.vector.scalar_tensor_tensor(neg_abs[:], e6[:], -1.0, e6[:], ALU.mult, ALU.min)
        nc.vector.scalar_tensor_tensor(front[:], e6[:], 0.0, n2[:], ALU.max, ALU.mult)

        inv_n, rs_w, inv_w = work("inv_n"), work("rs_w"), work("inv_w")
        nc.scalar.activation(inv_n[:], n_sq[:], ACT.Abs_reciprocal_sqrt, scale=0.225 * 0.225)
        nc.scalar.activation(rs_w[:], w6[:], ACT.Abs_reciprocal_sqrt, scale=2.5)
        nc.scalar.activation(inv_w[:], rs_w[:], ACT.Square)

        dist, rest, width, result = work("dist"), work("rest"), work("width"), work("result")
        nc.vector.tensor_tensor(dist[:], neg_abs[:], inv_n[:], ALU.mult)
        nc.vector.scalar_tensor_tensor(rest[:], dist[:], softness[:], n2[:], ALU.mult, ALU.add)
        halves = [slice(0, V // 2), slice(V // 2, V)]
        for cols in halves:
            nc.vector.tensor_tensor(width[:, cols], front[:, cols], inv_w[:, cols], ALU.mult)
        for cols in halves:
            nc.vector.scalar_tensor_tensor(result[:, cols], rest[:, cols], 0.075, width[:, cols], ALU.mult, ALU.add)
        nc.sync.dma_start(out, result[:])
